import numpy as np
import ml_dtypes


def mxq(x, axis, fmt="e4m3"):
    dtype, down = {"e4m3": (ml_dtypes.float8_e4m3fn, 7), "e5m2": (ml_dtypes.float8_e5m2, 14)}[fmt]
    v = np.moveaxis(np.asarray(x, np.float32).astype(ml_dtypes.bfloat16).astype(np.float64), axis, -1)
    blocks = v.reshape(v.shape[:-1] + (-1, 32))
    amax = np.abs(blocks).max(-1, keepdims=True)
    byte = np.maximum(np.where(amax > 0, np.frexp(amax)[1] - 1 + 127, 0) - down, 1)
    scale = np.exp2(byte - 127.0)
    codes = (blocks / scale).astype(np.float32).astype(dtype).astype(np.float64)
    return np.moveaxis((codes * scale).reshape(v.shape), -1, axis)


WIDE = False


def mx_kscale(k):
    if not WIDE:
        return np.ones(k)
    levels = np.array([10, -10, 5, -5, 0])
    if k % 512:
        return np.exp2(np.random.permutation(np.resize(levels, k // 32))).repeat(32)
    a = np.empty((k // 512, 16))
    for p in range(k // 512):
        a[p, :8] = np.random.permutation(np.resize(levels, 8))
        for g in range(8):
            far = levels[np.abs(levels - a[p, g]) >= 10]
            a[p, g + 8] = far[np.random.randint(len(far))]
    return np.exp2(a.ravel()).repeat(32)


def f64(x):
    return np.asarray(x).astype(np.float64)


def striped(idx):
    return np.tile(idx.reshape(-1, 16).T, (8, 1)).astype(np.uint16)


def unstriped(offs):
    return offs[:16].T.reshape(-1).astype(np.int64)


def gelu(v):
    return 0.5 * v * (1.0 + np.tanh(np.sqrt(2.0 / np.pi) * (v + 0.044715 * v**3)))

def planes(y):
    n, m = y.shape
    v = y.astype(np.float32).astype(ml_dtypes.bfloat16).astype(np.float64).reshape(n // 32, 32, m)
    top = np.abs(v).max(1)
    byte = np.clip(np.where(top > 0, np.frexp(top)[1] - 1 + 127 - 7, 1), 1, 254)
    codes = (v * np.exp2(127.0 - byte)[:, None, :]).reshape(n, m).astype(np.float32).astype(ml_dtypes.float8_e4m3fn).view(np.uint8)
    words = codes.reshape(n // 512, 128, 4, m).transpose(0, 1, 3, 2)
    return np.ascontiguousarray(words), np.ascontiguousarray(byte.astype(np.uint8).reshape(n // 512, 16, m))


K, T, S, V, H, J = 512, 2048, 1024, 512, 512, 512


def setup_inputs():
    n = np.random.standard_normal
    s = mx_kscale(K)[:, None]
    u = mx_kscale(H)
    r = mx_kscale(J)[:, None]
    return {
        "xT": (n((K, T)) * s).astype(np.float32),
        "eT": (n((J, V)) * r).astype(np.float32),
        "w1": (n((K, H)) / np.sqrt(3 * K) / s * u).astype(np.float32),
        "w2": (n((K, H)) / np.sqrt(3 * K) / s * u).astype(np.float32),
        "w3": (n((J, H)) / np.sqrt(3 * J) / r * u).astype(np.float32),
        "w4": (n((H, H)) / np.sqrt(H) / u[:, None]).astype(np.float32),
        "offs": striped(np.random.permutation(T)[:S]),
    }


def reference(xT, eT, w1, w2, w3, w4, offs):
    xq = mxq(f64(xT)[:, unstriped(offs)], 0, "e4m3")
    h = gelu(mxq(f64(w1), 0, "e4m3").T @ xq[:, :V] + mxq(f64(w2), 0, "e4m3").T @ xq[:, V:2 * V] + mxq(f64(w3), 0, "e4m3").T @ mxq(f64(eT), 0, "e4m3"))
    out_0 = mxq(f64(w4), 0, "e4m3").T @ mxq(h, 0, "e4m3")
    return (out_0,) + planes(out_0)

@@ -1,0 +1,165 @@
+from contextlib import ExitStack
+
+import concourse.mybir as mybir
+
+K, T, S, V, H = 512, 2048, 1024, 512, 512
+FLOPS = 4 * 2 * K * H * V
+
+F32 = mybir.dt.float32
+BF16 = mybir.dt.bfloat16
+U32 = mybir.dt.uint32
+I32 = mybir.dt.int32
+U16 = mybir.dt.uint16
+U8 = mybir.dt.uint8
+FP8X4 = mybir.dt.float8_e4m3fn_x4
+GELU = mybir.ActivationFunctionType.Gelu_apprx_tanh
+
+P = 128
+PACK = 4
+CHUNK = 128
+CHUNKS = V // CHUNK
+X_PIECES = (((0, 1024, "s"), (1024, 2048, "v")), ((0, 1024, "s"), (1024, 1536, "s"), (1536, 2048, "v")))
+
+
+def tile_picked_edgeup_gelu_lo_kernel(tc, xT, eT, w1, w2, w3, w4, offs, out_0, out_1, out_2):
+    nc = tc.nc
+
+    def copy(engine, out, in_):
+        if engine == "s":
+            nc.scalar.copy(out=out, in_=in_)
+        else:
+            nc.vector.tensor_copy(out=out, in_=in_)
+
+    with ExitStack() as ctx:
+        keep = ctx.enter_context(tc.tile_pool(name="keep", bufs=1))
+        psum = ctx.enter_context(tc.psum_pool(name="psum", bufs=1))
+
+        def operand(name, width, rounded=None):
+            if rounded is None:
+                rounded = keep.tile([P, PACK * width], BF16, name=name + "_bf16", align_bytes=64)
+            codes = keep.tile([P, width], U32, name=name + "_codes", align_bytes=64)
+            scales = keep.tile([P, width], U8, name=name + "_scales", align_bytes=64)
+            return rounded, codes, scales
+
+        def quantize(op, lo, hi):
+            rounded, codes, scales = op
+            nc.vector.quantize_mx(out=codes[:, lo:hi].bitcast(FP8X4), scales=scales[:, lo:hi], in_=rounded[:, PACK * lo : PACK * hi])
+
+        def product(bank, weights, moving, c, first, last):
+            cols = slice(c * CHUNK, (c + 1) * CHUNK)
+            for t in range(PACK):
+                rows = slice(t * P, (t + 1) * P)
+                nc.tensor.matmul_mx(
+                    out=bank[:, rows],
+                    lhsT=weights[1][:, rows].bitcast(FP8X4),
+                    lhsT_scale=weights[2][:, rows],
+                    rhs=moving[1][:, cols].bitcast(FP8X4),
+                    rhs_scale=moving[2][:, cols],
+                    start=first and t == 0,
+                    stop=last and t == PACK - 1,
+                )
+
+        x_rows = xT.rearrange("(p a e) n -> p a e n", a=2, e=2)
+        x_raw = {}
+        offsets = keep.tile([P, S // 16], U16, name="offsets")
+        for a in range(2):
+            for lo, hi, engine in X_PIECES[a]:
+                x_raw[a, lo] = keep.tile([P, 2, hi - lo], F32, name="x_raw_%d_%d" % (a, lo))
+                nc.sync.dma_start(out=x_raw[a, lo][:], in_=x_rows[:, a, :, lo:hi])
+            if a == 0:
+                nc.sync.dma_start(offsets[:], offs)
+        raw = {}
+        for name, rows in (("w1", w1), ("w2", w2), ("w3", w3), ("e", eT), ("w4", w4)):
+            raw[name] = keep.tile([P, PACK, 512], F32, name=name + "_raw")
+            nc.sync.dma_start(out=raw[name][:], in_=rows.rearrange("(p j) c -> p j c", j=PACK))
+
+        ends = [operand("src", V), operand("dst", V)]
+        picked = [keep.tile([P, 2, V], U32, name="picked_%d" % s) for s in range(2)]
+        for a in range(2):
+            pairs = keep.tile([P, 2 * T], BF16, name="pairs_%d" % a, align_bytes=64)
+            for lo, hi, engine in X_PIECES[a]:
+                copy(engine, pairs[:, 2 * lo : 2 * hi].rearrange("p (n e) -> p n e", e=2), x_raw[a, lo][:].rearrange("p e n -> p n e"))
+            for s in range(2):
+                nc.vector.tensor_copy(
+                    out=picked[s][:, a, :],
+                    in_=pairs[:].bitcast(U32).indirect(offsets[:, s * (V // 16) : (s + 1) * (V // 16)]),
+                )
+        for s in range(2):
+            nc.scalar.copy(out=ends[s][0][:].bitcast(U32).rearrange("p (n a) -> p n a", a=2), in_=picked[s][:].rearrange("p a n -> p n a"))
+
+        def deal_weights(name, op, engine, lo, hi):
+            copy(
+                engine,
+                op[0][:].rearrange("p (t m a e) -> p m a t e", t=PACK, a=2, e=2)[:, lo:hi],
+                raw[name][:].rearrange("p (a e) (m t) -> p m a t e", e=2, t=PACK)[:, lo:hi],
+            )
+
+        def interleave(engine, op, rows, lo, hi, first):
+            copy(
+                engine,
+                op[0][:, PACK * lo : PACK * hi].rearrange("p (c i j) -> p c j i", i=4, j=PACK),
+                rows[:, :, lo - first : hi - first].rearrange("p j (c i) -> p c j i", i=4),
+            )
+
+        q1, q2, q3 = [operand(name, H) for name in ("w1", "w2", "w3")]
+        edges, q4 = operand("e", V, q3[0]), operand("w4", H, q3[0])
+        hidden, result = operand("h", V), operand("y", V)
+        pre = [psum.tile([P, PACK * CHUNK], F32, name="pre_%d" % c) for c in range(CHUNKS)]
+        post = [psum.tile([P, PACK * CHUNK], F32, name="post_%d" % c) for c in range(CHUNKS)]
+
+        deal_weights("w1", q1, "v", 0, P)
+        quantize(ends[0], 0, V)
+        quantize(q1, 0, H)
+        for c in range(CHUNKS):
+            product(pre[c], q1, ends[0], c, True, False)
+        quantize(ends[1], 0, V)
+        deal_weights("w2", q2, "s", 0, P)
+        deal_weights("w3", q3, "s", 0, 56)
+        deal_weights("w3", q3, "v", 56, P)
+        quantize(q2, 0, H)
+        for c in range(CHUNKS):
+            product(pre[c], q2, ends[1], c, False, False)
+        quantize(q3, 0, H)
+
+        interleave("v", edges, raw["e"], 0, 128, 0)
+        interleave("v", edges, raw["e"], 128, 256, 0)
+        quantize(edges, 0, 128)
+        interleave("v", edges, raw["e"], 256, 512, 0)
+        quantize(edges, 128, 256)
+        quantize(edges, 256, 512)
+        for c in range(CHUNKS):
+            product(pre[c], q3, edges, c, False, True)
+            nc.scalar.activation(
+                out=hidden[0][:, PACK * c * CHUNK : PACK * (c + 1) * CHUNK].rearrange("p (n t) -> p n t", t=PACK),
+                in_=pre[c][:].rearrange("p (t n) -> p n t", t=PACK),
+                func=GELU,
+            )
+        deal_weights("w4", q4, "v", 0, P)
+        quantize(hidden, 0, 256)
+        quantize(q4, 0, H)
+        quantize(hidden, 256, 384)
+        quantize(hidden, 384, 512)
+
+        y_rows = out_0.rearrange("(p t) v -> p t v", t=PACK)
+        words = out_1.rearrange("z p c r -> p (z c r)").bitcast(I32)
+        for first, count in ((0, 2), (2, 1), (3, 1)):
+            base = first * CHUNK
+            y = keep.tile([P, PACK, count * CHUNK], F32, name="y_%d" % first)
+            for c in range(first, first + count):
+                product(post[c], q4, hidden, c, True, True)
+                if c == CHUNKS - 1:
+                    nc.vector.tensor_copy(
+                        out=result[0][:, PACK * c * CHUNK :].rearrange("p (n t) -> p n t", t=PACK),
+                        in_=post[c][:].rearrange("p (t n) -> p n t", t=PACK),
+                    )
+                nc.scalar.copy(out=y[:, :, c * CHUNK - base : (c + 1) * CHUNK - base], in_=post[c][:].rearrange("p (t n) -> p t n", t=PACK))
+                if c < CHUNKS - 1:
+                    interleave("v", result, y, c * CHUNK, (c + 1) * CHUNK, base)
+            nc.sync.dma_start(out=y_rows[:, :, base : base + count * CHUNK], in_=y[:])
+            if first == 0:
+                quantize(result, 0, 256)
+        quantize(result, 256, 512)
+        nc.sync.dma_start(out=words, in_=result[1][:].bitcast(I32))
+        for q in range(4):
+            queue = nc.scalar if q % 2 else nc.sync
+            queue.dma_start(out=out_2[0, 4 * q : 4 * q + 4, :].bitcast(I32), in_=result[2][32 * q : 32 * q + 4, :].bitcast(I32))

@@ -18,7 +18,10 @@ P = 128
 PACK = 4
 CHUNK = 128
 CHUNKS = V // CHUNK
-X_PIECES = (((0, 1024, "s"), (1024, 2048, "v")), ((0, 1024, "s"), (1024, 1536, "s"), (1536, 2048, "v")))
+X_PIECES = (
+    ((0, 1024, (("s", 0, 1024),)), (1024, 2048, (("v", 0, 704), ("s", 704, 1024)))),
+    ((0, 1024, (("s", 0, 1024),)), (1024, 1536, (("v", 0, 512),)), (1536, 2048, (("v", 0, 384), ("s", 384, 512)))),
+)
 
 
 def tile_picked_edgeup_gelu_lo_kernel(tc, xT, eT, w1, w2, w3, w4, offs, out_0, out_1, out_2):
@@ -34,10 +37,10 @@ def tile_picked_edgeup_gelu_lo_kernel(tc, xT, eT, w1, w2, w3, w4, offs, out_0, o
         keep = ctx.enter_context(tc.tile_pool(name="keep", bufs=1))
         psum = ctx.enter_context(tc.psum_pool(name="psum", bufs=1))
 
-        def operand(name, width, rounded=None):
+        def operand(name, width, rounded=None, after=None):
             if rounded is None:
                 rounded = keep.tile([P, PACK * width], BF16, name=name + "_bf16", align_bytes=64)
-            codes = keep.tile([P, width], U32, name=name + "_codes", align_bytes=64)
+            codes = keep.tile([P, width], U32, name=name + "_codes", tag=after or name + "_codes", align_bytes=64)
             scales = keep.tile([P, width], U8, name=name + "_scales", align_bytes=64)
             return rounded, codes, scales
 
@@ -59,6 +62,11 @@ def tile_picked_edgeup_gelu_lo_kernel(tc, xT, eT, w1, w2, w3, w4, offs, out_0, o
                     stop=last and t == PACK - 1,
                 )
 
+        warm_in = keep.tile([P, 1], F32, name="warm_in")
+        warm_out = keep.tile([P, 1], F32, name="warm_out")
+        nc.vector.memset(warm_in[:], 0.0)
+        nc.scalar.activation(out=warm_out[:], in_=warm_in[:], func=GELU)
+
         x_rows = xT.rearrange("(p a e) n -> p a e n", a=2, e=2)
         x_raw = {}
         offsets = keep.tile([P, S // 16], U16, name="offsets")
@@ -70,15 +78,21 @@ def tile_picked_edgeup_gelu_lo_kernel(tc, xT, eT, w1, w2, w3, w4, offs, out_0, o
                 nc.sync.dma_start(offsets[:], offs)
         raw = {}
         for name, rows in (("w1", w1), ("w2", w2), ("w3", w3), ("e", eT), ("w4", w4)):
-            raw[name] = keep.tile([P, PACK, 512], F32, name=name + "_raw")
+            raw[name] = keep.tile([P, PACK, 512], F32, name=name + "_raw", align_bytes=64)
             nc.sync.dma_start(out=raw[name][:], in_=rows.rearrange("(p j) c -> p j c", j=PACK))
 
-        ends = [operand("src", V), operand("dst", V)]
+        q1, q2, q3 = [operand(name, H) for name in ("w1", "w2", "w3")]
+        ends = [operand("src", V, after="w1_raw"), operand("dst", V, after="w1_bf16")]
         picked = [keep.tile([P, 2, V], U32, name="picked_%d" % s) for s in range(2)]
         for a in range(2):
             pairs = keep.tile([P, 2 * T], BF16, name="pairs_%d" % a, align_bytes=64)
-            for lo, hi, engine in X_PIECES[a]:
-                copy(engine, pairs[:, 2 * lo : 2 * hi].rearrange("p (n e) -> p n e", e=2), x_raw[a, lo][:].rearrange("p e n -> p n e"))
+            for lo, hi, shares in X_PIECES[a]:
+                for engine, first, last in shares:
+                    copy(
+                        engine,
+                        pairs[:, 2 * (lo + first) : 2 * (lo + last)].rearrange("p (n e) -> p n e", e=2),
+                        x_raw[a, lo][:, :, first:last].rearrange("p e n -> p n e"),
+                    )
             for s in range(2):
                 nc.vector.tensor_copy(
                     out=picked[s][:, a, :],
@@ -90,8 +104,8 @@ def tile_picked_edgeup_gelu_lo_kernel(tc, xT, eT, w1, w2, w3, w4, offs, out_0, o
         def deal_weights(name, op, engine, lo, hi):
             copy(
                 engine,
-                op[0][:].rearrange("p (t m a e) -> p m a t e", t=PACK, a=2, e=2)[:, lo:hi],
-                raw[name][:].rearrange("p (a e) (m t) -> p m a t e", e=2, t=PACK)[:, lo:hi],
+                op[0][:].rearrange("p (t m a e) -> p m a t e", t=PACK, a=2, e=2)[:, :, :, lo:hi],
+                raw[name][:].rearrange("p (a e) (m t) -> p m a t e", e=2, t=PACK)[:, :, :, lo:hi],
             )
 
         def interleave(engine, op, rows, lo, hi, first):
@@ -101,62 +115,64 @@ def tile_picked_edgeup_gelu_lo_kernel(tc, xT, eT, w1, w2, w3, w4, offs, out_0, o
                 rows[:, :, lo - first : hi - first].rearrange("p j (c i) -> p c j i", i=4),
             )
 
-        q1, q2, q3 = [operand(name, H) for name in ("w1", "w2", "w3")]
         edges, q4 = operand("e", V, q3[0]), operand("w4", H, q3[0])
-        hidden, result = operand("h", V), operand("y", V)
+        result = operand("y", V)
+        h_first, h_rest = operand("h_first", CHUNK, after="w4_raw"), operand("h_rest", V - CHUNK, after="w3_bf16")
+        hidden = [(h_first, 0)] + [(h_rest, c) for c in range(CHUNKS - 1)]
         pre = [psum.tile([P, PACK * CHUNK], F32, name="pre_%d" % c) for c in range(CHUNKS)]
         post = [psum.tile([P, PACK * CHUNK], F32, name="post_%d" % c) for c in range(CHUNKS)]
 
-        deal_weights("w1", q1, "v", 0, P)
+        deal_weights("w1", q1, "v", 0, 4)
         quantize(ends[0], 0, V)
         quantize(q1, 0, H)
         for c in range(CHUNKS):
             product(pre[c], q1, ends[0], c, True, False)
         quantize(ends[1], 0, V)
-        deal_weights("w2", q2, "s", 0, P)
-        deal_weights("w3", q3, "s", 0, 56)
-        deal_weights("w3", q3, "v", 56, P)
+        deal_weights("w2", q2, "s", 0, 4)
+        deal_weights("w3", q3, "s", 0, 2)
+        deal_weights("w3", q3, "v", 2, 4)
         quantize(q2, 0, H)
         for c in range(CHUNKS):
             product(pre[c], q2, ends[1], c, False, False)
         quantize(q3, 0, H)
 
         interleave("v", edges, raw["e"], 0, 128, 0)
+        interleave("s", edges, raw["e"], 256, 384, 0)
         interleave("v", edges, raw["e"], 128, 256, 0)
+        interleave("s", edges, raw["e"], 384, 512, 0)
         quantize(edges, 0, 128)
-        interleave("v", edges, raw["e"], 256, 512, 0)
         quantize(edges, 128, 256)
         quantize(edges, 256, 512)
         for c in range(CHUNKS):
             product(pre[c], q3, edges, c, False, True)
             nc.scalar.activation(
-                out=hidden[0][:, PACK * c * CHUNK : PACK * (c + 1) * CHUNK].rearrange("p (n t) -> p n t", t=PACK),
+                out=hidden[c][0][0][:, PACK * hidden[c][1] * CHUNK : PACK * (hidden[c][1] + 1) * CHUNK].rearrange("p (n t) -> p n t", t=PACK),
                 in_=pre[c][:].rearrange("p (t n) -> p n t", t=PACK),
                 func=GELU,
             )
-        deal_weights("w4", q4, "v", 0, P)
-        quantize(hidden, 0, 256)
-        quantize(q4, 0, H)
-        quantize(hidden, 256, 384)
-        quantize(hidden, 384, 512)
+        deal_weights("w4", q4, "v", 0, 4)
+        quantize(h_first, 0, CHUNK)
+        quantize(q4, 0, H // 2)
+        quantize(q4, H // 2, H)
+        for c in range(CHUNKS - 1):
+            quantize(h_rest, c * CHUNK, (c + 1) * CHUNK)
 
         y_rows = out_0.rearrange("(p t) v -> p t v", t=PACK)
         words = out_1.rearrange("z p c r -> p (z c r)").bitcast(I32)
-        for first, count in ((0, 2), (2, 1), (3, 1)):
-            base = first * CHUNK
-            y = keep.tile([P, PACK, count * CHUNK], F32, name="y_%d" % first)
-            for c in range(first, first + count):
-                product(post[c], q4, hidden, c, True, True)
-                if c == CHUNKS - 1:
-                    nc.vector.tensor_copy(
-                        out=result[0][:, PACK * c * CHUNK :].rearrange("p (n t) -> p n t", t=PACK),
-                        in_=post[c][:].rearrange("p (t n) -> p n t", t=PACK),
-                    )
-                nc.scalar.copy(out=y[:, :, c * CHUNK - base : (c + 1) * CHUNK - base], in_=post[c][:].rearrange("p (t n) -> p t n", t=PACK))
-                if c < CHUNKS - 1:
-                    interleave("v", result, y, c * CHUNK, (c + 1) * CHUNK, base)
-            nc.sync.dma_start(out=y_rows[:, :, base : base + count * CHUNK], in_=y[:])
-            if first == 0:
+        for c in range(CHUNKS):
+            base = c * CHUNK
+            y = keep.tile([P, PACK, CHUNK], F32, name="y_%d" % c)
+            product(post[c], q4, hidden[c][0], hidden[c][1], True, True)
+            if c == CHUNKS - 1:
+                nc.vector.tensor_copy(
+                    out=result[0][:, PACK * c * CHUNK :].rearrange("p (n t) -> p n t", t=PACK),
+                    in_=post[c][:].rearrange("p (t n) -> p n t", t=PACK),
+                )
+            nc.scalar.copy(out=y[:], in_=post[c][:].rearrange("p (t n) -> p t n", t=PACK))
+            nc.sync.dma_start(out=y_rows[:, :, base : base + CHUNK], in_=y[:])
+            if c < CHUNKS - 1:
+                interleave("v", result, y, base, base + CHUNK, base)
+            if c == 1:
                 quantize(result, 0, 256)
         quantize(result, 256, 512)
         nc.sync.dma_start(out=words, in_=result[1][:].bitcast(I32))

@@ -90,8 +90,8 @@ def tile_picked_edgeup_gelu_lo_kernel(tc, xT, eT, w1, w2, w3, w4, offs, out_0, o
                 for engine, first, last in shares:
                     copy(
                         engine,
-                        pairs[:, 2 * (lo + first) : 2 * (lo + last)].rearrange("p (n e) -> p n e", e=2),
-                        x_raw[a, lo][:, :, first:last].rearrange("p e n -> p n e"),
+                        pairs[:, 2 * (lo + first) : 2 * (lo + last)].rearrange("p (c i e) -> p c e i", i=4, e=2),
+                        x_raw[a, lo][:, :, first:last].rearrange("p e (c i) -> p c e i", i=4),
                     )
             for s in range(2):
                 nc.vector.tensor_copy(
@@ -99,13 +99,13 @@ def tile_picked_edgeup_gelu_lo_kernel(tc, xT, eT, w1, w2, w3, w4, offs, out_0, o
                     in_=pairs[:].bitcast(U32).indirect(offsets[:, s * (V // 16) : (s + 1) * (V // 16)]),
                 )
         for s in range(2):
-            nc.scalar.copy(out=ends[s][0][:].bitcast(U32).rearrange("p (n a) -> p n a", a=2), in_=picked[s][:].rearrange("p a n -> p n a"))
+            nc.scalar.copy(out=ends[s][0][:].bitcast(U32).rearrange("p (c i a) -> p c a i", i=4, a=2), in_=picked[s][:].rearrange("p a (c i) -> p c a i", i=4))
 
         def deal_weights(name, op, engine, lo, hi):
             copy(
                 engine,
-                op[0][:].rearrange("p (t m a e) -> p m a t e", t=PACK, a=2, e=2)[:, :, :, lo:hi],
-                raw[name][:].rearrange("p (a e) (m t) -> p m a t e", e=2, t=PACK)[:, :, :, lo:hi],
+                op[0][:].rearrange("p (t m j) -> p m j t", t=PACK, j=PACK)[:, :, :, lo:hi],
+                raw[name][:].rearrange("p j (m t) -> p m j t", t=PACK)[:, :, :, lo:hi],
             )
 
         def interleave(engine, op, rows, lo, hi, first):
@@ -146,8 +146,8 @@ def tile_picked_edgeup_gelu_lo_kernel(tc, xT, eT, w1, w2, w3, w4, offs, out_0, o
         for c in range(CHUNKS):
             product(pre[c], q3, edges, c, False, True)
             nc.scalar.activation(
-                out=hidden[c][0][0][:, PACK * hidden[c][1] * CHUNK : PACK * (hidden[c][1] + 1) * CHUNK].rearrange("p (n t) -> p n t", t=PACK),
-                in_=pre[c][:].rearrange("p (t n) -> p n t", t=PACK),
+                out=hidden[c][0][0][:, PACK * hidden[c][1] * CHUNK : PACK * (hidden[c][1] + 1) * CHUNK].rearrange("p (c i t) -> p c t i", i=4, t=PACK),
+                in_=pre[c][:].rearrange("p (t c i) -> p c t i", i=4, t=PACK),
                 func=GELU,
             )
         deal_weights("w4", q4, "v", 0, 4)
@@ -165,8 +165,8 @@ def tile_picked_edgeup_gelu_lo_kernel(tc, xT, eT, w1, w2, w3, w4, offs, out_0, o
             product(post[c], q4, hidden[c][0], hidden[c][1], True, True)
             if c == CHUNKS - 1:
                 nc.vector.tensor_copy(
-                    out=result[0][:, PACK * c * CHUNK :].rearrange("p (n t) -> p n t", t=PACK),
-                    in_=post[c][:].rearrange("p (t n) -> p n t", t=PACK),
+                    out=result[0][:, PACK * c * CHUNK :].rearrange("p (c i t) -> p c t i", i=4, t=PACK),
+                    in_=post[c][:].rearrange("p (t c i) -> p c t i", i=4, t=PACK),
                 )
             nc.scalar.copy(out=y[:], in_=post[c][:].rearrange("p (t n) -> p t n", t=PACK))
             nc.sync.dma_start(out=y_rows[:, :, base : base + CHUNK], in_=y[:])

@@ -18,10 +18,12 @@ P = 128
 PACK = 4
 CHUNK = 128
 CHUNKS = V // CHUNK
-X_PIECES = (
-    ((0, 1024, (("s", 0, 1024),)), (1024, 2048, (("v", 0, 704), ("s", 704, 1024)))),
-    ((0, 1024, (("s", 0, 1024),)), (1024, 1536, (("v", 0, 512),)), (1536, 2048, (("v", 0, 384), ("s", 384, 512)))),
+X_LOADS = (((0, 1024), (1024, T)), ((0, 1024), (1024, 1536), (1536, T)))
+X_CASTS = (
+    (("s", 0, 0, 1024), ("v", 1024, 1024, 1728), ("s", 1024, 1728, T)),
+    (("s", 0, 0, 1024), ("v", 1024, 1024, 1536), ("v", 1536, 1536, 1920), ("s", 1536, 1920, T)),
 )
+Y_STORES = ((0, 1), (1, 2), (3, 1))
 
 
 def tile_picked_edgeup_gelu_lo_kernel(tc, xT, eT, w1, w2, w3, w4, offs, out_0, out_1, out_2):
@@ -37,9 +39,8 @@ def tile_picked_edgeup_gelu_lo_kernel(tc, xT, eT, w1, w2, w3, w4, offs, out_0, o
         keep = ctx.enter_context(tc.tile_pool(name="keep", bufs=1))
         psum = ctx.enter_context(tc.psum_pool(name="psum", bufs=1))
 
-        def operand(name, width, rounded=None, after=None):
-            if rounded is None:
-                rounded = keep.tile([P, PACK * width], BF16, name=name + "_bf16", align_bytes=64)
+        def operand(name, width, after=None, rounded_after=None):
+            rounded = keep.tile([P, PACK * width], BF16, name=name + "_bf16", tag=rounded_after or name + "_bf16", align_bytes=64)
             codes = keep.tile([P, width], U32, name=name + "_codes", tag=after or name + "_codes", align_bytes=64)
             scales = keep.tile([P, width], U8, name=name + "_scales", align_bytes=64)
             return rounded, codes, scales
@@ -62,16 +63,11 @@ def tile_picked_edgeup_gelu_lo_kernel(tc, xT, eT, w1, w2, w3, w4, offs, out_0, o
                     stop=last and t == PACK - 1,
                 )
 
-        warm_in = keep.tile([P, 1], F32, name="warm_in")
-        warm_out = keep.tile([P, 1], F32, name="warm_out")
-        nc.vector.memset(warm_in[:], 0.0)
-        nc.scalar.activation(out=warm_out[:], in_=warm_in[:], func=GELU)
-
         x_rows = xT.rearrange("(p a e) n -> p a e n", a=2, e=2)
         x_raw = {}
         offsets = keep.tile([P, S // 16], U16, name="offsets")
         for a in range(2):
-            for lo, hi, engine in X_PIECES[a]:
+            for lo, hi in X_LOADS[a]:
                 x_raw[a, lo] = keep.tile([P, 2, hi - lo], F32, name="x_raw_%d_%d" % (a, lo))
                 nc.sync.dma_start(out=x_raw[a, lo][:], in_=x_rows[:, a, :, lo:hi])
             if a == 0:
@@ -86,26 +82,25 @@ def tile_picked_edgeup_gelu_lo_kernel(tc, xT, eT, w1, w2, w3, w4, offs, out_0, o
         picked = [keep.tile([P, 2, V], U32, name="picked_%d" % s) for s in range(2)]
         for a in range(2):
             pairs = keep.tile([P, 2 * T], BF16, name="pairs_%d" % a, align_bytes=64)
-            for lo, hi, shares in X_PIECES[a]:
-                for engine, first, last in shares:
-                    copy(
-                        engine,
-                        pairs[:, 2 * (lo + first) : 2 * (lo + last)].rearrange("p (c i e) -> p c e i", i=4, e=2),
-                        x_raw[a, lo][:, :, first:last].rearrange("p e (c i) -> p c e i", i=4),
-                    )
+            for engine, piece, lo, hi in X_CASTS[a]:
+                copy(
+                    engine,
+                    pairs[:, 2 * lo : 2 * hi].rearrange("p (n e) -> p n e", e=2),
+                    x_raw[a, piece][:, :, lo - piece : hi - piece].rearrange("p e n -> p n e"),
+                )
             for s in range(2):
                 nc.vector.tensor_copy(
                     out=picked[s][:, a, :],
                     in_=pairs[:].bitcast(U32).indirect(offsets[:, s * (V // 16) : (s + 1) * (V // 16)]),
                 )
         for s in range(2):
-            nc.scalar.copy(out=ends[s][0][:].bitcast(U32).rearrange("p (c i a) -> p c a i", i=4, a=2), in_=picked[s][:].rearrange("p a (c i) -> p c a i", i=4))
+            nc.scalar.copy(out=ends[s][0][:].bitcast(U32).rearrange("p (n a) -> p n a", a=2), in_=picked[s][:].rearrange("p a n -> p n a"))
 
         def deal_weights(name, op, engine, lo, hi):
             copy(
                 engine,
-                op[0][:].rearrange("p (t m j) -> p m j t", t=PACK, j=PACK)[:, :, :, lo:hi],
-                raw[name][:].rearrange("p j (m t) -> p m j t", t=PACK)[:, :, :, lo:hi],
+                op[0][:].rearrange("p (t m a e) -> p m a t e", t=PACK, a=2, e=2)[:, :, :, lo:hi],
+                raw[name][:].rearrange("p (a e) (m t) -> p m a t e", e=2, t=PACK)[:, :, :, lo:hi],
             )
 
         def interleave(engine, op, rows, lo, hi, first):
@@ -115,9 +110,9 @@ def tile_picked_edgeup_gelu_lo_kernel(tc, xT, eT, w1, w2, w3, w4, offs, out_0, o
                 rows[:, :, lo - first : hi - first].rearrange("p j (c i) -> p c j i", i=4),
             )
 
-        edges, q4 = operand("e", V, q3[0]), operand("w4", H, q3[0])
+        edges, q4 = operand("e", V), operand("w4", H, rounded_after="e_bf16")
         result = operand("y", V)
-        h_first, h_rest = operand("h_first", CHUNK, after="w4_raw"), operand("h_rest", V - CHUNK, after="w3_bf16")
+        h_first, h_rest = operand("h_first", CHUNK, after="w4_raw"), operand("h_rest", V - CHUNK, after="e_bf16")
         hidden = [(h_first, 0)] + [(h_rest, c) for c in range(CHUNKS - 1)]
         pre = [psum.tile([P, PACK * CHUNK], F32, name="pre_%d" % c) for c in range(CHUNKS)]
         post = [psum.tile([P, PACK * CHUNK], F32, name="post_%d" % c) for c in range(CHUNKS)]
@@ -137,43 +132,46 @@ def tile_picked_edgeup_gelu_lo_kernel(tc, xT, eT, w1, w2, w3, w4, offs, out_0, o
         quantize(q3, 0, H)
 
         interleave("v", edges, raw["e"], 0, 128, 0)
-        interleave("s", edges, raw["e"], 256, 384, 0)
-        interleave("v", edges, raw["e"], 128, 256, 0)
         interleave("s", edges, raw["e"], 384, 512, 0)
+        interleave("v", edges, raw["e"], 128, 256, 0)
         quantize(edges, 0, 128)
+        interleave("v", edges, raw["e"], 256, 384, 0)
         quantize(edges, 128, 256)
         quantize(edges, 256, 512)
         for c in range(CHUNKS):
             product(pre[c], q3, edges, c, False, True)
             nc.scalar.activation(
-                out=hidden[c][0][0][:, PACK * hidden[c][1] * CHUNK : PACK * (hidden[c][1] + 1) * CHUNK].rearrange("p (c i t) -> p c t i", i=4, t=PACK),
-                in_=pre[c][:].rearrange("p (t c i) -> p c t i", i=4, t=PACK),
+                out=hidden[c][0][0][:, PACK * hidden[c][1] * CHUNK : PACK * (hidden[c][1] + 1) * CHUNK].rearrange("p (n t) -> p n t", t=PACK),
+                in_=pre[c][:].rearrange("p (t n) -> p n t", t=PACK),
                 func=GELU,
             )
-        deal_weights("w4", q4, "v", 0, 4)
+            if c == 0:
+                deal_weights("w4", q4, "v", 0, 4)
         quantize(h_first, 0, CHUNK)
         quantize(q4, 0, H // 2)
         quantize(q4, H // 2, H)
-        for c in range(CHUNKS - 1):
-            quantize(h_rest, c * CHUNK, (c + 1) * CHUNK)
+        quantize(h_rest, 0, 2 * CHUNK)
+        quantize(h_rest, 2 * CHUNK, 3 * CHUNK)
 
         y_rows = out_0.rearrange("(p t) v -> p t v", t=PACK)
         words = out_1.rearrange("z p c r -> p (z c r)").bitcast(I32)
-        for c in range(CHUNKS):
-            base = c * CHUNK
-            y = keep.tile([P, PACK, CHUNK], F32, name="y_%d" % c)
-            product(post[c], q4, hidden[c][0], hidden[c][1], True, True)
-            if c == CHUNKS - 1:
-                nc.vector.tensor_copy(
-                    out=result[0][:, PACK * c * CHUNK :].rearrange("p (c i t) -> p c t i", i=4, t=PACK),
-                    in_=post[c][:].rearrange("p (t c i) -> p c t i", i=4, t=PACK),
-                )
-            nc.scalar.copy(out=y[:], in_=post[c][:].rearrange("p (t n) -> p t n", t=PACK))
-            nc.sync.dma_start(out=y_rows[:, :, base : base + CHUNK], in_=y[:])
-            if c < CHUNKS - 1:
-                interleave("v", result, y, base, base + CHUNK, base)
-            if c == 1:
-                quantize(result, 0, 256)
+        for first, count in Y_STORES:
+            base = first * CHUNK
+            y = keep.tile([P, PACK, count * CHUNK], F32, name="y_%d" % first)
+            for c in range(first, first + count):
+                product(post[c], q4, hidden[c][0], hidden[c][1], True, True)
+                if c == CHUNKS - 1:
+                    nc.vector.tensor_copy(
+                        out=result[0][:, PACK * c * CHUNK :].rearrange("p (n t) -> p n t", t=PACK),
+                        in_=post[c][:].rearrange("p (t n) -> p n t", t=PACK),
+                    )
+                copy("s", y[:, :, c * CHUNK - base : (c + 1) * CHUNK - base], post[c][:].rearrange("p (t n) -> p t n", t=PACK))
+                if c == first + count - 1:
+                    nc.sync.dma_start(out=y_rows[:, :, base : base + count * CHUNK], in_=y[:])
+                if c < CHUNKS - 1:
+                    interleave("v", result, y, c * CHUNK, (c + 1) * CHUNK, base)
+                if c == 1:
+                    quantize(result, 0, 256)
         quantize(result, 256, 512)
         nc.sync.dma_start(out=words, in_=result[1][:].bitcast(I32))
         for q in range(4):

from contextlib import ExitStack

import concourse.mybir as mybir

K, T, S, V, H = 512, 2048, 1024, 512, 512
FLOPS = 4 * 2 * K * H * V

F32 = mybir.dt.float32
BF16 = mybir.dt.bfloat16
U32 = mybir.dt.uint32
I32 = mybir.dt.int32
U16 = mybir.dt.uint16
U8 = mybir.dt.uint8
FP8X4 = mybir.dt.float8_e4m3fn_x4
GELU = mybir.ActivationFunctionType.Gelu_apprx_tanh

P = 128
PACK = 4
CHUNK = 128
CHUNKS = V // CHUNK
X_LOADS = (((0, 1024), (1024, T)), ((0, 1024), (1024, 1536), (1536, T)))
X_CASTS = (
    (("s", 0, 0, 1024), ("v", 1024, 1024, 1728), ("s", 1024, 1728, T)),
    (("s", 0, 0, 1024), ("v", 1024, 1024, 1536), ("v", 1536, 1536, 1920), ("s", 1536, 1920, T)),
)
Y_STORES = ((0, 1), (1, 2), (3, 1))


def tile_picked_edgeup_gelu_lo_kernel(tc, xT, eT, w1, w2, w3, w4, offs, out_0, out_1, out_2):
    nc = tc.nc

    def copy(engine, out, in_):
        if engine == "s":
            nc.scalar.copy(out=out, in_=in_)
        else:
            nc.vector.tensor_copy(out=out, in_=in_)

    with ExitStack() as ctx:
        keep = ctx.enter_context(tc.tile_pool(name="keep", bufs=1))
        psum = ctx.enter_context(tc.psum_pool(name="psum", bufs=1))

        def operand(name, width, after=None, rounded_after=None):
            rounded = keep.tile([P, PACK * width], BF16, name=name + "_bf16", tag=rounded_after or name + "_bf16", align_bytes=64)
            codes = keep.tile([P, width], U32, name=name + "_codes", tag=after or name + "_codes", align_bytes=64)
            scales = keep.tile([P, width], U8, name=name + "_scales", align_bytes=64)
            return rounded, codes, scales

        def quantize(op, lo, hi):
            rounded, codes, scales = op
            nc.vector.quantize_mx(out=codes[:, lo:hi].bitcast(FP8X4), scales=scales[:, lo:hi], in_=rounded[:, PACK * lo : PACK * hi])

        def product(bank, weights, moving, c, first, last):
            cols = slice(c * CHUNK, (c + 1) * CHUNK)
            for t in range(PACK):
                rows = slice(t * P, (t + 1) * P)
                nc.tensor.matmul_mx(
                    out=bank[:, rows],
                    lhsT=weights[1][:, rows].bitcast(FP8X4),
                    lhsT_scale=weights[2][:, rows],
                    rhs=moving[1][:, cols].bitcast(FP8X4),
                    rhs_scale=moving[2][:, cols],
                    start=first and t == 0,
                    stop=last and t == PACK - 1,
                )

        x_rows = xT.rearrange("(p a e) n -> p a e n", a=2, e=2)
        x_raw = {}
        offsets = keep.tile([P, S // 16], U16, name="offsets")
        for a in range(2):
            for lo, hi in X_LOADS[a]:
                x_raw[a, lo] = keep.tile([P, 2, hi - lo], F32, name="x_raw_%d_%d" % (a, lo))
                nc.sync.dma_start(out=x_raw[a, lo][:], in_=x_rows[:, a, :, lo:hi])
            if a == 0:
                nc.sync.dma_start(offsets[:], offs)
        raw = {}
        for name, rows in (("w1", w1), ("w2", w2), ("w3", w3), ("e", eT), ("w4", w4)):
            raw[name] = keep.tile([P, PACK, 512], F32, name=name + "_raw", align_bytes=64)
            nc.sync.dma_start(out=raw[name][:], in_=rows.rearrange("(p j) c -> p j c", j=PACK))

        q1, q2, q3 = [operand(name, H) for name in ("w1", "w2", "w3")]
        ends = [operand("src", V, after="w1_raw"), operand("dst", V, after="w1_bf16")]
        picked = [keep.tile([P, 2, V], U32, name="picked_%d" % s) for s in range(2)]
        for a in range(2):
            pairs = keep.tile([P, 2 * T], BF16, name="pairs_%d" % a, align_bytes=64)
            for engine, piece, lo, hi in X_CASTS[a]:
                copy(
                    engine,
                    pairs[:, 2 * lo : 2 * hi].rearrange("p (n e) -> p n e", e=2),
                    x_raw[a, piece][:, :, lo - piece : hi - piece].rearrange("p e n -> p n e"),
                )
            for s in range(2):
                nc.vector.tensor_copy(
                    out=picked[s][:, a, :],
                    in_=pairs[:].bitcast(U32).indirect(offsets[:, s * (V // 16) : (s + 1) * (V // 16)]),
                )
        for s in range(2):
            nc.scalar.copy(out=ends[s][0][:].bitcast(U32).rearrange("p (n a) -> p n a", a=2), in_=picked[s][:].rearrange("p a n -> p n a"))

        def deal_weights(name, op, engine, lo, hi):
            copy(
                engine,
                op[0][:].rearrange("p (t m a e) -> p m a t e", t=PACK, a=2, e=2)[:, :, :, lo:hi],
                raw[name][:].rearrange("p (a e) (m t) -> p m a t e", e=2, t=PACK)[:, :, :, lo:hi],
            )

        def interleave(engine, op, rows, lo, hi, first):
            copy(
                engine,
                op[0][:, PACK * lo : PACK * hi].rearrange("p (c i j) -> p c j i", i=4, j=PACK),
                rows[:, :, lo - first : hi - first].rearrange("p j (c i) -> p c j i", i=4),
            )

        edges, q4 = operand("e", V), operand("w4", H, rounded_after="e_bf16")
        result = operand("y", V)
        h_first, h_rest = operand("h_first", CHUNK, after="w4_raw"), operand("h_rest", V - CHUNK, after="e_bf16")
        hidden = [(h_first, 0)] + [(h_rest, c) for c in range(CHUNKS - 1)]
        pre = [psum.tile([P, PACK * CHUNK], F32, name="pre_%d" % c) for c in range(CHUNKS)]
        post = [psum.tile([P, PACK * CHUNK], F32, name="post_%d" % c) for c in range(CHUNKS)]

        deal_weights("w1", q1, "v", 0, 4)
        quantize(ends[0], 0, V)
        quantize(q1, 0, H)
        for c in range(CHUNKS):
            product(pre[c], q1, ends[0], c, True, False)
        quantize(ends[1], 0, V)
        deal_weights("w2", q2, "s", 0, 4)
        deal_weights("w3", q3, "s", 0, 2)
        deal_weights("w3", q3, "v", 2, 4)
        quantize(q2, 0, H)
        for c in range(CHUNKS):
            product(pre[c], q2, ends[1], c, False, False)
        quantize(q3, 0, H)

        interleave("v", edges, raw["e"], 0, 128, 0)
        interleave("s", edges, raw["e"], 384, 512, 0)
        interleave("v", edges, raw["e"], 128, 256, 0)
        quantize(edges, 0, 128)
        interleave("v", edges, raw["e"], 256, 384, 0)
        quantize(edges, 128, 256)
        quantize(edges, 256, 512)
        for c in range(CHUNKS):
            product(pre[c], q3, edges, c, False, True)
            nc.scalar.activation(
                out=hidden[c][0][0][:, PACK * hidden[c][1] * CHUNK : PACK * (hidden[c][1] + 1) * CHUNK].rearrange("p (n t) -> p n t", t=PACK),
                in_=pre[c][:].rearrange("p (t n) -> p n t", t=PACK),
                func=GELU,
            )
            if c == 0:
                deal_weights("w4", q4, "v", 0, 4)
        quantize(h_first, 0, CHUNK)
        quantize(q4, 0, H // 2)
        quantize(q4, H // 2, H)
        quantize(h_rest, 0, 2 * CHUNK)
        quantize(h_rest, 2 * CHUNK, 3 * CHUNK)

        y_rows = out_0.rearrange("(p t) v -> p t v", t=PACK)
        words = out_1.rearrange("z p c r -> p (z c r)").bitcast(I32)
        for first, count in Y_STORES:
            base = first * CHUNK
            y = keep.tile([P, PACK, count * CHUNK], F32, name="y_%d" % first)
            for c in range(first, first + count):
                product(post[c], q4, hidden[c][0], hidden[c][1], True, True)
                if c == CHUNKS - 1:
                    nc.vector.tensor_copy(
                        out=result[0][:, PACK * c * CHUNK :].rearrange("p (n t) -> p n t", t=PACK),
                        in_=post[c][:].rearrange("p (t n) -> p n t", t=PACK),
                    )
                copy("s", y[:, :, c * CHUNK - base : (c + 1) * CHUNK - base], post[c][:].rearrange("p (t n) -> p t n", t=PACK))
                if c == first + count - 1:
                    nc.sync.dma_start(out=y_rows[:, :, base : base + count * CHUNK], in_=y[:])
                if c < CHUNKS - 1:
                    interleave("v", result, y, c * CHUNK, (c + 1) * CHUNK, base)
                if c == 1:
                    quantize(result, 0, 256)
        quantize(result, 256, 512)
        nc.sync.dma_start(out=words, in_=result[1][:].bitcast(I32))
        for q in range(4):
            queue = nc.scalar if q % 2 else nc.sync
            queue.dma_start(out=out_2[0, 4 * q : 4 * q + 4, :].bitcast(I32), in_=result[2][32 * q : 32 * q + 4, :].bitcast(I32))
